import numpy as np
import ml_dtypes


def mxq(x, axis, fmt="e4m3"):
    dtype, down = {"e4m3": (ml_dtypes.float8_e4m3fn, 7), "e5m2": (ml_dtypes.float8_e5m2, 14)}[fmt]
    v = np.moveaxis(np.asarray(x, np.float32).astype(ml_dtypes.bfloat16).astype(np.float64), axis, -1)
    blocks = v.reshape(v.shape[:-1] + (-1, 32))
    amax = np.abs(blocks).max(-1, keepdims=True)
    byte = np.maximum(np.where(amax > 0, np.frexp(amax)[1] - 1 + 127, 0) - down, 1)
    scale = np.exp2(byte - 127.0)
    codes = (blocks / scale).astype(np.float32).astype(dtype).astype(np.float64)
    return np.moveaxis((codes * scale).reshape(v.shape), -1, axis)


WIDE = False


def mx_kscale(k):
    if not WIDE:
        return np.ones(k)
    levels = np.array([10, -10, 5, -5, 0])
    if k % 512:
        return np.exp2(np.random.permutation(np.resize(levels, k // 32))).repeat(32)
    a = np.empty((k // 512, 16))
    for p in range(k // 512):
        a[p, :8] = np.random.permutation(np.resize(levels, 8))
        for g in range(8):
            far = levels[np.abs(levels - a[p, g]) >= 10]
            a[p, g + 8] = far[np.random.randint(len(far))]
    return np.exp2(a.ravel()).repeat(32)


def f64(x):
    return np.asarray(x).astype(np.float64)


def striped(idx):
    return np.tile(idx.reshape(-1, 16).T, (8, 1)).astype(np.uint16)


def unstriped(offs):
    return offs[:16].T.reshape(-1).astype(np.int64)


def striped8(idx):
    return np.concatenate([x.reshape(-1, 16).T for x in idx]).astype(np.uint16)


def runs(offs, k):
    lists = np.stack([offs[16 * r : 16 * r + 16].T.reshape(-1) for r in range(8)]).astype(np.int64)
    return lists[np.arange(k) % 512 // 64]


def pack_weight(w):
    k, n = w.shape
    w = f64(np.asarray(w, np.float32).astype(ml_dtypes.bfloat16)).reshape(k // 32, 32, n)
    amax = np.abs(w).max(1)
    byte = np.clip(np.where(amax > 0, np.frexp(amax)[1] - 1 + 127 - 7, 1), 1, 254)
    scaled = (w * np.exp2(127.0 - byte)[:, None, :]).reshape(k, n).astype(np.float32)
    words = np.ascontiguousarray(scaled.reshape(k // 512, 128, 4, n).transpose(0, 1, 3, 2)).astype(ml_dtypes.float8_e4m3fn).view(np.uint8)
    return words, np.ascontiguousarray(byte.astype(np.uint8).reshape(k // 512, 16, n))


def unpack_weight(words, scales):
    g, p, n, _ = words.shape
    vals = np.ascontiguousarray(words).view(ml_dtypes.float8_e4m3fn).astype(np.float64) * np.repeat(np.exp2(scales.astype(np.float64) - 127.0), 8, axis=1)[..., None]
    return vals.transpose(0, 1, 3, 2).reshape(g * 512, n)


def sigmoid(v):
    return 1.0 / (1.0 + np.exp(-np.maximum(v, -700.0)))


K, T, S, V, G, H = 512, 1024, 512, 512, 2048, 512


def setup_inputs():
    n = np.random.standard_normal
    s = mx_kscale(K)[:, None]
    u = mx_kscale(S)
    packed_xT = pack_weight(n((K, T)) * s)
    packed_dT = pack_weight(n((K, G)) / s)
    return {
        "x_words": packed_xT[0],
        "x_scales": packed_xT[1],
        "d_words": packed_dT[0],
        "d_scales": packed_dT[1],
        "w1": (n((K, H)) / np.sqrt(K) / s).astype(np.float32),
        "ga": (np.random.uniform(0.5, 1.5, (H, 1)) * u[:, None]).astype(np.float32),
        "gb": (np.random.uniform(0.5, 1.5, (H, 1)) / u[:, None]).astype(np.float32),
        "offs": striped(np.random.permutation(T)[:S]),
        "k1": striped8(np.random.randint(0, G, (8, H))),
        "two": striped(np.random.permutation(T)[:V]),
        "n1": striped8(np.stack([np.random.permutation(S) for _ in range(8)])),
        "n2": striped8(np.stack([np.random.permutation(V) for _ in range(8)])),
        "n3": striped8(np.stack([np.random.permutation(V) for _ in range(8)])),
        "n4": striped8(np.stack([np.random.permutation(V) for _ in range(8)])),
        "n5": striped8(np.stack([np.random.permutation(V) for _ in range(8)])),
        "n6": striped8(np.stack([np.random.permutation(V) for _ in range(8)])),
    }


def reference(x_words, x_scales, d_words, d_scales, w1, ga, gb, offs, k1, two, n1, n2, n3, n4, n5, n6):
    d_k1 = unpack_weight(d_words, d_scales)[np.arange(K)[:, None], runs(k1, K)]
    xq = unpack_weight(x_words, x_scales)[:, unstriped(offs)]
    a = 0.0625 * (d_k1.T @ xq)
    z = f64(ga) * (a * (sigmoid(a[np.arange(H)[:, None], runs(n1, H)])))
    x_two = unpack_weight(x_words, x_scales)[:, unstriped(two)]
    b = mxq(f64(w1), 0, "e4m3").T @ x_two
    z2 = f64(gb) * (b * (b[np.arange(H)[:, None], runs(n2, H)] - (b[np.arange(H)[:, None], runs(n3, H)])))
    s = 0.0625 * ((mxq(z, 0, "e4m3").T @ mxq(z2, 0, "e4m3")))
    return np.maximum(s, s[np.arange(S)[:, None], runs(n4, S)]) - (np.maximum(s[np.arange(S)[:, None], runs(n5, S)], s[np.arange(S)[:, None], runs(n6, S)]))

@@ -1,0 +1,199 @@
+from contextlib import ExitStack
+
+import concourse.mybir as mybir
+
+F32 = mybir.dt.float32
+BF16 = mybir.dt.bfloat16
+I32 = mybir.dt.int32
+U32 = mybir.dt.uint32
+U16 = mybir.dt.uint16
+U8 = mybir.dt.uint8
+FP8X4 = mybir.dt.float8_e4m3fn_x4
+ALU = mybir.AluOpType
+ACT = mybir.ActivationFunctionType
+
+P = 128
+PACK = 4
+K, T, S, G = 512, 1024, 512, 2048
+SIXTEENTH = 0.0625
+PIECES = [(0, 256), (256, 384), (384, 512)]
+FLOPS = 3 * 2 * 512 * 512 * 512
+
+
+def tile_picked_ckqgatewindmix_none_p_kernel(
+    tc, x_words, x_scales, d_words, d_scales, w1, ga, gb, offs, k1, two, n1, n2, n3, n4, n5, n6, out
+):
+    nc = tc.nc
+    with ExitStack() as ctx:
+        lists = ctx.enter_context(tc.tile_pool(name="lists", bufs=1))
+        keep = ctx.enter_context(tc.tile_pool(name="keep", bufs=1))
+        psum = ctx.enter_context(tc.psum_pool(name="psum", bufs=1))
+
+        def tile(name, shape, dtype):
+            return keep.tile(shape, dtype, name=name, align_bytes=64)
+
+        def load_list(name, src):
+            held = lists.tile([P, S // 16], U16, name=name)
+            nc.sync.dma_start(held[:], src)
+            return held
+
+        def mx(acc, lhs, lhs_scale, rhs, rhs_scale):
+            nc.tensor.matmul_mx(acc, lhsT=lhs.bitcast(FP8X4), lhsT_scale=lhs_scale, rhs=rhs.bitcast(FP8X4), rhs_scale=rhs_scale, start=True, stop=True)
+
+        banks = [psum.tile([P, S], F32, name="bank%d" % i) for i in range(8)]
+
+        xs_win = tile("xs_win", [P, T], U8)
+        ds_win = tile("ds_win", [P, G], U8)
+        nc.vector.memset(xs_win[:].bitcast(I32), 0)
+        nc.vector.memset(ds_win[:].bitcast(I32), 0)
+        two_l = load_list("two_l", two)
+        xw_win = tile("xw_win", [P, T], U32)
+        nc.sync.dma_start(xw_win[:].bitcast(I32), x_words[0].rearrange("p n t -> p (n t)").bitcast(I32))
+        for q in range(4):
+            nc.scalar.dma_start(xs_win[32 * q : 32 * q + 4, :].bitcast(I32), x_scales[0, 4 * q : 4 * q + 4, :].bitcast(I32))
+        w_rows = w1.rearrange("(p j) c -> p j c", j=PACK)
+        w_raw = [tile("w_raw%d" % h, [P, PACK, 256], F32) for h in range(2)]
+        for h in range(2):
+            nc.sync.dma_start(w_raw[h][:], w_rows[:, :, 256 * h : 256 * (h + 1)])
+        k1_l = load_list("k1_l", k1)
+        nc.scalar.dma_start(ds_win[0:P:8, :].bitcast(I32), d_scales[0].bitcast(I32))
+        offs_l = load_list("offs_l", offs)
+        dw_win = tile("dw_win", [P, G], U32)
+        nc.sync.dma_start(dw_win[:].bitcast(I32), d_words[0].rearrange("p n t -> p (n t)").bitcast(I32))
+        n3_l = load_list("n3_l", n3)
+        n2_l = load_list("n2_l", n2)
+        gb_t = tile("gb_t", [P, PACK], F32)
+        nc.sync.dma_start(gb_t[:], gb.rearrange("(p t) o -> p (t o)", t=PACK))
+        n1_l = load_list("n1_l", n1)
+        ga_t = tile("ga_t", [P, PACK], F32)
+        nc.sync.dma_start(ga_t[:], ga.rearrange("(p t) o -> p (t o)", t=PACK))
+        n4_l = load_list("n4_l", n4)
+        n5_l = load_list("n5_l", n5)
+        n6_l = load_list("n6_l", n6)
+
+        ds_plane = tile("ds_plane", [P, S], U8)
+        nc.gpsimd.memset(ds_plane[:].bitcast(I32), 0)
+        wide = [tile("wide%d" % t, [P, 2 * S], F32) for t in range(PACK)]
+        for t in range(PACK):
+            nc.gpsimd.memset(wide[t][:, S:], 0.0)
+
+        x2_w = tile("x2_w", [P, S], U32)
+        x2_s = tile("x2_s", [P, S], U8)
+        nc.vector.tensor_copy(x2_w[:], xw_win[:].indirect(two_l[:]))
+        nc.vector.tensor_copy(x2_s[:], xs_win[:].indirect(two_l[:]))
+
+        w_bf = tile("w_bf", [P, PACK * K], BF16)
+        w_view = w_bf[:].rearrange("p (t m j) -> p m t j", t=PACK, j=PACK)
+        for h in range(2):
+            nc.scalar.copy(w_view[:, 64 * h : 64 * (h + 1), :, :], w_raw[h][:].rearrange("p j (m t) -> p m t j", t=PACK))
+
+        dk_s = tile("dk_s", [P, S], U8)
+        dk_s_dealt = tile("dk_s_dealt", [P, S], U8)
+        nc.vector.tensor_copy(dk_s[:], ds_win[:].indirect(k1_l[:]))
+        x1_w = tile("x1_w", [P, S], U32)
+        x1_s = tile("x1_s", [P, S], U8)
+        nc.vector.tensor_copy(x1_w[:], xw_win[:].indirect(offs_l[:]))
+        nc.vector.tensor_copy(dk_s_dealt[:].rearrange("p (t m) -> p m t", t=PACK), dk_s[:].rearrange("p (m t) -> p m t", t=PACK))
+        for q in range(4):
+            nc.sync.dma_start(ds_plane[32 * q : 32 * q + 4, :].bitcast(I32), dk_s_dealt[32 * q : 32 * q + 32 : 8, :].bitcast(I32))
+        nc.vector.tensor_copy(x1_s[:], xs_win[:].indirect(offs_l[:]))
+
+        w_q = tile("w_q", [P, K], U32)
+        w_s = tile("w_s", [P, K], U8)
+        nc.vector.quantize_mx(w_q[:].bitcast(FP8X4), w_s[:], w_bf[:])
+        b_win = [tile("b_win%d" % t, [P, S], F32) for t in range(PACK)]
+        for t in range(PACK):
+            cols = slice(P * t, P * (t + 1))
+            mx(banks[t][:], w_q[:, cols], w_s[:, cols], x2_w[:], x2_s[:])
+            nc.scalar.copy(b_win[t][:], banks[t][:])
+
+        dk_w = tile("dk_w", [P, S], U32)
+        dk_w_dealt = tile("dk_w_dealt", [P, S], U32)
+        nc.vector.tensor_copy(dk_w[:], dw_win[:].indirect(k1_l[:]))
+        nc.vector.tensor_copy(dk_w_dealt[:].rearrange("p (t m) -> p m t", t=PACK), dk_w[:].rearrange("p (m t) -> p m t", t=PACK))
+        sig = [tile("sig%d" % t, [P, S], F32) for t in range(PACK)]
+        for t in range(PACK):
+            cols = slice(P * t, P * (t + 1))
+            mx(banks[4 + t][:], dk_w_dealt[:, cols], ds_plane[:, cols], x1_w[:], x1_s[:])
+            nc.scalar.activation(wide[t][:, :S], banks[4 + t][:], ACT.Copy, scale=SIXTEENTH)
+            nc.scalar.activation(sig[t][:], wide[t][:].indirect(n1_l[:]), ACT.Sigmoid)
+
+        z2_q, z2_s = [], []
+
+        def z2_piece(n):
+            lo, hi = PIECES[n]
+            width = hi - lo
+            entries = slice(lo // 16, hi // 16)
+            planes = tile("z2_planes%d" % n, [P, PACK, width], BF16)
+            far = [tile("far%d_%d" % (n, t), [P, width], F32) for t in range(PACK)]
+            diff = [tile("diff%d_%d" % (n, t), [P, width], F32) for t in range(PACK)]
+            for step in range(PACK + 2):
+                if step < PACK:
+                    nc.vector.tensor_copy(far[step][:], b_win[step][:].indirect(n3_l[:, entries]))
+                if 1 <= step < PACK + 1:
+                    t = step - 1
+                    nc.vector.tensor_tensor(diff[t][:], b_win[t][:].indirect(n2_l[:, entries]), far[t][:], ALU.subtract)
+                if step >= 2:
+                    t = step - 2
+                    nc.vector.scalar_tensor_tensor(planes[:, t, :], b_win[t][:, lo:hi], gb_t[:, t : t + 1], diff[t][:], ALU.mult, ALU.mult)
+            woven = tile("z2_woven%d" % n, [P, width * PACK], BF16)
+            woven_view = woven[:].rearrange("p (c t) -> p c t", t=PACK)
+            if n == len(PIECES) - 1:
+                nc.vector.tensor_copy(woven_view, planes[:].rearrange("p t c -> p c t"))
+            else:
+                nc.scalar.copy(woven_view, planes[:].rearrange("p t c -> p c t"))
+            z2_q.append(tile("z2_q%d" % n, [P, width], U32))
+            z2_s.append(tile("z2_s%d" % n, [P, width], U8))
+            return woven
+
+        def z2_quantise(n, woven):
+            nc.vector.quantize_mx(z2_q[n][:].bitcast(FP8X4), z2_s[n][:], woven[:])
+
+        woven0 = z2_piece(0)
+        z_planes = tile("z_planes", [P, PACK, S], BF16)
+        for t in range(PACK):
+            nc.vector.scalar_tensor_tensor(z_planes[:, t, :], wide[t][:, :S], ga_t[:, t : t + 1], sig[t][:], ALU.mult, ALU.mult)
+        z_woven = [tile("z_woven%d" % u, [P, P * PACK], BF16) for u in range(PACK)]
+        z_cols = z_planes[:].rearrange("p t (m u) -> p u m t", u=PACK)
+        for u in range(PACK):
+            nc.scalar.copy(z_woven[u][:].rearrange("p (m t) -> p m t", t=PACK), z_cols[:, u, :, :])
+        woven1 = z2_piece(1)
+        z2_quantise(0, woven0)
+        z_q = [tile("z_q%d" % u, [P, P], U32) for u in range(PACK)]
+        z_s = [tile("z_s%d" % u, [P, P], U8) for u in range(PACK)]
+        nc.vector.quantize_mx(z_q[0][:].bitcast(FP8X4), z_s[0][:], z_woven[0][:])
+        z2_quantise(1, woven1)
+        for n in range(2):
+            lo, hi = PIECES[n]
+            mx(banks[0][:, lo:hi], z_q[0][:], z_s[0][:], z2_q[n][:], z2_s[n][:])
+        last = PIECES[-1][0]
+        nc.scalar.activation(wide[0][:, :last], banks[0][:, :last], ACT.Copy, scale=-SIXTEENTH)
+        woven2 = z2_piece(2)
+        z2_quantise(2, woven2)
+        mx(banks[0][:, last:], z_q[0][:], z_s[0][:], z2_q[2][:], z2_s[2][:])
+        nc.scalar.activation(wide[0][:, last:S], banks[0][:, last:], ACT.Copy, scale=-SIXTEENTH)
+        for u in range(1, PACK):
+            nc.vector.quantize_mx(z_q[u][:].bitcast(FP8X4), z_s[u][:], z_woven[u][:])
+            for n in range(len(PIECES)):
+                lo, hi = PIECES[n]
+                mx(banks[u][:, lo:hi], z_q[u][:], z_s[u][:], z2_q[n][:], z2_s[n][:])
+            nc.scalar.activation(wide[u][:, :S], banks[u][:], ACT.Copy, scale=-SIXTEENTH)
+
+        out_rows = out.rearrange("(p u) v -> p u v", u=PACK)
+        g4 = [tile("g4_%d" % u, [P, S], F32) for u in range(PACK)]
+        low = [tile("low%d" % u, [P, S], F32) for u in range(PACK)]
+        v5 = [tile("v5_%d" % u, [P, S], F32) for u in range(PACK)]
+        v6 = [tile("v6_%d" % u, [P, S], F32) for u in range(PACK)]
+        res = [tile("res%d" % u, [P, S], F32) for u in range(PACK)]
+        for step in range(PACK + 1):
+            if step < PACK:
+                nc.vector.tensor_copy(g4[step][:], wide[step][:].indirect(n4_l[:]))
+            if step >= 1:
+                u = step - 1
+                nc.vector.tensor_tensor(v5[u][:], wide[u][:].indirect(n5_l[:]), low[u][:], ALU.subtract)
+            if step < PACK:
+                nc.vector.tensor_tensor(low[step][:], wide[step][:, :S], g4[step][:], ALU.min)
+            if step >= 1:
+                nc.vector.tensor_tensor(v6[u][:], wide[u][:].indirect(n6_l[:]), low[u][:], ALU.subtract)
+                nc.vector.tensor_tensor(res[u][:], v5[u][:], v6[u][:], ALU.min)
+                nc.sync.dma_start(out_rows[:, u, :], res[u][:])

@@ -1,6 +1,7 @@
 from contextlib import ExitStack
 
 import concourse.mybir as mybir
+from concourse.masks import make_identity
 
 F32 = mybir.dt.float32
 BF16 = mybir.dt.bfloat16
@@ -16,7 +17,8 @@ P = 128
 PACK = 4
 K, T, S, G = 512, 1024, 512, 2048
 SIXTEENTH = 0.0625
-PIECES = [(0, 256), (256, 384), (384, 512)]
+PIECES = [(0, 256), (256, 512)]
+RUN = 8
 FLOPS = 3 * 2 * 512 * 512 * 512
 
 
@@ -44,133 +46,143 @@ def tile_picked_ckqgatewindmix_none_p_kernel(
 
         xs_win = tile("xs_win", [P, T], U8)
         ds_win = tile("ds_win", [P, G], U8)
-        nc.vector.memset(xs_win[:].bitcast(I32), 0)
-        nc.vector.memset(ds_win[:].bitcast(I32), 0)
+        nc.gpsimd.memset(ds_win[:].bitcast(I32), 0)
+        nc.gpsimd.memset(xs_win[:].bitcast(I32), 0)
         two_l = load_list("two_l", two)
         xw_win = tile("xw_win", [P, T], U32)
         nc.sync.dma_start(xw_win[:].bitcast(I32), x_words[0].rearrange("p n t -> p (n t)").bitcast(I32))
-        for q in range(4):
-            nc.scalar.dma_start(xs_win[32 * q : 32 * q + 4, :].bitcast(I32), x_scales[0, 4 * q : 4 * q + 4, :].bitcast(I32))
-        w_rows = w1.rearrange("(p j) c -> p j c", j=PACK)
-        w_raw = [tile("w_raw%d" % h, [P, PACK, 256], F32) for h in range(2)]
-        for h in range(2):
-            nc.sync.dma_start(w_raw[h][:], w_rows[:, :, 256 * h : 256 * (h + 1)])
+        nc.sync.dma_start(ds_win[0:P:8, :].bitcast(I32), d_scales[0].bitcast(I32))
         k1_l = load_list("k1_l", k1)
-        nc.scalar.dma_start(ds_win[0:P:8, :].bitcast(I32), d_scales[0].bitcast(I32))
+        for q in range(4):
+            nc.sync.dma_start(xs_win[32 * q : 32 * q + 4, :].bitcast(I32), x_scales[0, 4 * q : 4 * q + 4, :].bitcast(I32))
+        w_raw = tile("w_raw", [P, PACK, K], F32)
+        nc.sync.dma_start(w_raw[:], w1.rearrange("(p j) c -> p j c", j=PACK))
         offs_l = load_list("offs_l", offs)
         dw_win = tile("dw_win", [P, G], U32)
         nc.sync.dma_start(dw_win[:].bitcast(I32), d_words[0].rearrange("p n t -> p (n t)").bitcast(I32))
         n3_l = load_list("n3_l", n3)
         n2_l = load_list("n2_l", n2)
-        gb_t = tile("gb_t", [P, PACK], F32)
-        nc.sync.dma_start(gb_t[:], gb.rearrange("(p t) o -> p (t o)", t=PACK))
+        gain_rows = tile("gain_rows", [P, P], F32)
+        nc.gpsimd.memset(gain_rows[:], 0.0)
+        for i, gain in enumerate((ga, gb)):
+            nc.sync.dma_start(
+                gain_rows[PACK * i : PACK * (i + 1), :].rearrange("t (b r) -> t b r", r=RUN),
+                gain.rearrange("(b t r) o -> t b (r o)", t=PACK, r=RUN),
+            )
         n1_l = load_list("n1_l", n1)
-        ga_t = tile("ga_t", [P, PACK], F32)
-        nc.sync.dma_start(ga_t[:], ga.rearrange("(p t) o -> p (t o)", t=PACK))
         n4_l = load_list("n4_l", n4)
         n5_l = load_list("n5_l", n5)
         n6_l = load_list("n6_l", n6)
 
         ds_plane = tile("ds_plane", [P, S], U8)
         nc.gpsimd.memset(ds_plane[:].bitcast(I32), 0)
+        identity = tile("identity", [P, P], F32)
+        make_identity(nc, identity[:])
         wide = [tile("wide%d" % t, [P, 2 * S], F32) for t in range(PACK)]
-        for t in range(PACK):
-            nc.gpsimd.memset(wide[t][:, S:], 0.0)
-
-        x2_w = tile("x2_w", [P, S], U32)
-        x2_s = tile("x2_s", [P, S], U8)
-        nc.vector.tensor_copy(x2_w[:], xw_win[:].indirect(two_l[:]))
-        nc.vector.tensor_copy(x2_s[:], xs_win[:].indirect(two_l[:]))
-
-        w_bf = tile("w_bf", [P, PACK * K], BF16)
-        w_view = w_bf[:].rearrange("p (t m j) -> p m t j", t=PACK, j=PACK)
-        for h in range(2):
-            nc.scalar.copy(w_view[:, 64 * h : 64 * (h + 1), :, :], w_raw[h][:].rearrange("p j (m t) -> p m t j", t=PACK))
+        a_win = wide[: PACK - 1] + [tile("a_last", [P, 2 * S], F32)]
+        for window in a_win + wide[PACK - 1 :]:
+            nc.gpsimd.memset(window[:, S:], 0.0)
 
         dk_s = tile("dk_s", [P, S], U8)
         dk_s_dealt = tile("dk_s_dealt", [P, S], U8)
-        nc.vector.tensor_copy(dk_s[:], ds_win[:].indirect(k1_l[:]))
+        x2_w = tile("x2_w", [P, S], U32)
+        x2_s = tile("x2_s", [P, S], U8)
         x1_w = tile("x1_w", [P, S], U32)
         x1_s = tile("x1_s", [P, S], U8)
-        nc.vector.tensor_copy(x1_w[:], xw_win[:].indirect(offs_l[:]))
-        nc.vector.tensor_copy(dk_s_dealt[:].rearrange("p (t m) -> p m t", t=PACK), dk_s[:].rearrange("p (m t) -> p m t", t=PACK))
+        nc.vector.tensor_copy(x2_w[:], xw_win[:].indirect(two_l[:]))
+        nc.vector.tensor_copy(dk_s[:], ds_win[:].indirect(k1_l[:]))
+        nc.vector.tensor_copy(x2_s[:], xs_win[:].indirect(two_l[:]))
+        nc.vector.tensor_copy(
+            dk_s_dealt[:].bitcast(I32).rearrange("p (t b r) -> p t b r", t=PACK, r=RUN // 4),
+            dk_s[:].bitcast(I32).rearrange("p (b t r) -> p t b r", t=PACK, r=RUN // 4),
+        )
         for q in range(4):
             nc.sync.dma_start(ds_plane[32 * q : 32 * q + 4, :].bitcast(I32), dk_s_dealt[32 * q : 32 * q + 32 : 8, :].bitcast(I32))
+        nc.vector.tensor_copy(x1_w[:], xw_win[:].indirect(offs_l[:]))
         nc.vector.tensor_copy(x1_s[:], xs_win[:].indirect(offs_l[:]))
 
-        w_q = tile("w_q", [P, K], U32)
-        w_s = tile("w_s", [P, K], U8)
-        nc.vector.quantize_mx(w_q[:].bitcast(FP8X4), w_s[:], w_bf[:])
+        w_cols = w_raw[:].rearrange("p j (b t r) -> p t b r j", t=PACK, r=RUN)
         b_win = [tile("b_win%d" % t, [P, S], F32) for t in range(PACK)]
+        w_bf = [tile("w_bf%d" % t, [P, PACK * P], BF16) for t in range(PACK)]
         for t in range(PACK):
-            cols = slice(P * t, P * (t + 1))
-            mx(banks[t][:], w_q[:, cols], w_s[:, cols], x2_w[:], x2_s[:])
+            nc.scalar.copy(w_bf[t][:].rearrange("p (b r j) -> p b r j", r=RUN, j=PACK), w_cols[:, t, :, :, :])
+        for t in range(PACK):
+            w_q = tile("w_q%d" % t, [P, P], U32)
+            w_s = tile("w_s%d" % t, [P, P], U8)
+            nc.vector.quantize_mx(w_q[:].bitcast(FP8X4), w_s[:], w_bf[t][:])
+            mx(banks[t][:], w_q[:], w_s[:], x2_w[:], x2_s[:])
             nc.scalar.copy(b_win[t][:], banks[t][:])
+
+        gains = tile("gains", [P, 2 * PACK], F32)
+        nc.tensor.transpose(banks[7][:, :P], gain_rows[:], identity[:])
+        nc.scalar.copy(gains[:], banks[7][:, : 2 * PACK])
 
         dk_w = tile("dk_w", [P, S], U32)
         dk_w_dealt = tile("dk_w_dealt", [P, S], U32)
         nc.vector.tensor_copy(dk_w[:], dw_win[:].indirect(k1_l[:]))
-        nc.vector.tensor_copy(dk_w_dealt[:].rearrange("p (t m) -> p m t", t=PACK), dk_w[:].rearrange("p (m t) -> p m t", t=PACK))
+        nc.vector.tensor_copy(
+            dk_w_dealt[:].rearrange("p (t b r) -> p t b r", t=PACK, r=RUN),
+            dk_w[:].rearrange("p (b t r) -> p t b r", t=PACK, r=RUN),
+        )
         sig = [tile("sig%d" % t, [P, S], F32) for t in range(PACK)]
         for t in range(PACK):
             cols = slice(P * t, P * (t + 1))
             mx(banks[4 + t][:], dk_w_dealt[:, cols], ds_plane[:, cols], x1_w[:], x1_s[:])
-            nc.scalar.activation(wide[t][:, :S], banks[4 + t][:], ACT.Copy, scale=SIXTEENTH)
-            nc.scalar.activation(sig[t][:], wide[t][:].indirect(n1_l[:]), ACT.Sigmoid)
+            nc.scalar.activation(a_win[t][:, :S], banks[4 + t][:], ACT.Copy, scale=SIXTEENTH)
+            nc.scalar.activation(sig[t][:], a_win[t][:].indirect(n1_l[:]), ACT.Sigmoid)
 
         z2_q, z2_s = [], []
 
-        def z2_piece(n):
+        def z2_piece(n, far, diff, woven):
             lo, hi = PIECES[n]
             width = hi - lo
             entries = slice(lo // 16, hi // 16)
             planes = tile("z2_planes%d" % n, [P, PACK, width], BF16)
-            far = [tile("far%d_%d" % (n, t), [P, width], F32) for t in range(PACK)]
-            diff = [tile("diff%d_%d" % (n, t), [P, width], F32) for t in range(PACK)]
             for step in range(PACK + 2):
                 if step < PACK:
-                    nc.vector.tensor_copy(far[step][:], b_win[step][:].indirect(n3_l[:, entries]))
+                    nc.vector.tensor_copy(far[step], b_win[step][:].indirect(n3_l[:, entries]))
                 if 1 <= step < PACK + 1:
                     t = step - 1
-                    nc.vector.tensor_tensor(diff[t][:], b_win[t][:].indirect(n2_l[:, entries]), far[t][:], ALU.subtract)
+                    nc.vector.tensor_tensor(diff[t], b_win[t][:].indirect(n2_l[:, entries]), far[t], ALU.subtract)
                 if step >= 2:
                     t = step - 2
-                    nc.vector.scalar_tensor_tensor(planes[:, t, :], b_win[t][:, lo:hi], gb_t[:, t : t + 1], diff[t][:], ALU.mult, ALU.mult)
-            woven = tile("z2_woven%d" % n, [P, width * PACK], BF16)
-            woven_view = woven[:].rearrange("p (c t) -> p c t", t=PACK)
+                    nc.vector.scalar_tensor_tensor(planes[:, t, :], b_win[t][:, lo:hi], gains[:, PACK + t : PACK + t + 1], diff[t], ALU.mult, ALU.mult)
+            woven_view = woven.rearrange("p (c t) -> p c t", t=PACK)
             if n == len(PIECES) - 1:
                 nc.vector.tensor_copy(woven_view, planes[:].rearrange("p t c -> p c t"))
             else:
                 nc.scalar.copy(woven_view, planes[:].rearrange("p t c -> p c t"))
             z2_q.append(tile("z2_q%d" % n, [P, width], U32))
             z2_s.append(tile("z2_s%d" % n, [P, width], U8))
-            return woven
 
         def z2_quantise(n, woven):
-            nc.vector.quantize_mx(z2_q[n][:].bitcast(FP8X4), z2_s[n][:], woven[:])
+            nc.vector.quantize_mx(z2_q[n][:].bitcast(FP8X4), z2_s[n][:], woven)
 
-        woven0 = z2_piece(0)
+        def scratch(name, width):
+            return [tile("%s%d" % (name, t), [P, width], F32)[:] for t in range(PACK)]
+
+        woven0 = a_win[PACK - 1][:, S:].bitcast(BF16)
+        z2_piece(0, scratch("far_a", 256), scratch("diff_a", 256), woven0)
         z_planes = tile("z_planes", [P, PACK, S], BF16)
         for t in range(PACK):
-            nc.vector.scalar_tensor_tensor(z_planes[:, t, :], wide[t][:, :S], ga_t[:, t : t + 1], sig[t][:], ALU.mult, ALU.mult)
+            nc.vector.scalar_tensor_tensor(z_planes[:, t, :], a_win[t][:, :S], gains[:, t : t + 1], sig[t][:], ALU.mult, ALU.mult)
         z_woven = [tile("z_woven%d" % u, [P, P * PACK], BF16) for u in range(PACK)]
         z_cols = z_planes[:].rearrange("p t (m u) -> p u m t", u=PACK)
         for u in range(PACK):
             nc.scalar.copy(z_woven[u][:].rearrange("p (m t) -> p m t", t=PACK), z_cols[:, u, :, :])
-        woven1 = z2_piece(1)
         z2_quantise(0, woven0)
         z_q = [tile("z_q%d" % u, [P, P], U32) for u in range(PACK)]
         z_s = [tile("z_s%d" % u, [P, P], U8) for u in range(PACK)]
         nc.vector.quantize_mx(z_q[0][:].bitcast(FP8X4), z_s[0][:], z_woven[0][:])
-        z2_quantise(1, woven1)
-        for n in range(2):
-            lo, hi = PIECES[n]
-            mx(banks[0][:, lo:hi], z_q[0][:], z_s[0][:], z2_q[n][:], z2_s[n][:])
         last = PIECES[-1][0]
+        mx(banks[0][:, :last], z_q[0][:], z_s[0][:], z2_q[0][:], z2_s[0][:])
         nc.scalar.activation(wide[0][:, :last], banks[0][:, :last], ACT.Copy, scale=-SIXTEENTH)
-        woven2 = z2_piece(2)
-        z2_quantise(2, woven2)
-        mx(banks[0][:, last:], z_q[0][:], z_s[0][:], z2_q[2][:], z2_s[2][:])
+        far_c = [sig[t][:, 0:256] for t in range(PACK)]
+        diff_c = [sig[t][:, 256:512] for t in range(PACK - 1)] + [z_woven[0][:].bitcast(F32)]
+        woven1 = tile("z2_woven1", [P, 256 * PACK], BF16)[:]
+        z2_piece(1, far_c, diff_c, woven1)
+        z2_quantise(1, woven1)
+        mx(banks[0][:, last:], z_q[0][:], z_s[0][:], z2_q[1][:], z2_s[1][:])
         nc.scalar.activation(wide[0][:, last:S], banks[0][:, last:], ACT.Copy, scale=-SIXTEENTH)
         for u in range(1, PACK):
             nc.vector.quantize_mx(z_q[u][:].bitcast(FP8X4), z_s[u][:], z_woven[u][:])
@@ -185,15 +197,32 @@ def tile_picked_ckqgatewindmix_none_p_kernel(
         v5 = [tile("v5_%d" % u, [P, S], F32) for u in range(PACK)]
         v6 = [tile("v6_%d" % u, [P, S], F32) for u in range(PACK)]
         res = [tile("res%d" % u, [P, S], F32) for u in range(PACK)]
-        for step in range(PACK + 1):
-            if step < PACK:
-                nc.vector.tensor_copy(g4[step][:], wide[step][:].indirect(n4_l[:]))
-            if step >= 1:
-                u = step - 1
-                nc.vector.tensor_tensor(v5[u][:], wide[u][:].indirect(n5_l[:]), low[u][:], ALU.subtract)
-            if step < PACK:
-                nc.vector.tensor_tensor(low[step][:], wide[step][:, :S], g4[step][:], ALU.min)
-            if step >= 1:
-                nc.vector.tensor_tensor(v6[u][:], wide[u][:].indirect(n6_l[:]), low[u][:], ALU.subtract)
-                nc.vector.tensor_tensor(res[u][:], v5[u][:], v6[u][:], ALU.min)
-                nc.sync.dma_start(out_rows[:, u, :], res[u][:])
+
+        def first_pair_gather(u):
+            nc.vector.tensor_copy(g4[u][:], wide[u][:].indirect(n4_l[:]))
+
+        def first_pair_min(u):
+            nc.vector.tensor_tensor(low[u][:], wide[u][:, :S], g4[u][:], ALU.min)
+
+        def against(dst, list_tile, u, lo, hi):
+            nc.vector.tensor_tensor(dst[u][:, lo:hi], wide[u][:].indirect(list_tile[:, lo // 16 : hi // 16]), low[u][:, lo:hi], ALU.subtract)
+
+        def finish(u, lo, hi):
+            nc.vector.tensor_tensor(res[u][:, lo:hi], v5[u][:, lo:hi], v6[u][:, lo:hi], ALU.min)
+            nc.sync.dma_start(out_rows[:, u, lo:hi], res[u][:, lo:hi])
+
+        first_pair_gather(0)
+        first_pair_min(0)
+        for u in range(PACK - 1):
+            against(v5, n5_l, u, 0, S)
+            first_pair_gather(u + 1)
+            against(v6, n6_l, u, 0, S)
+            first_pair_min(u + 1)
+            finish(u, 0, S)
+        u, half = PACK - 1, S // 2
+        against(v5, n5_l, u, 0, half)
+        against(v6, n6_l, u, 0, half)
+        against(v5, n5_l, u, half, S)
+        finish(u, 0, half)
+        against(v6, n6_l, u, half, S)
+        finish(u, half, S)

@@ -176,53 +176,51 @@ def tile_picked_ckqgatewindmix_none_p_kernel(
         nc.vector.quantize_mx(z_q[0][:].bitcast(FP8X4), z_s[0][:], z_woven[0][:])
         last = PIECES[-1][0]
         mx(banks[0][:, :last], z_q[0][:], z_s[0][:], z2_q[0][:], z2_s[0][:])
-        nc.scalar.activation(wide[0][:, :last], banks[0][:, :last], ACT.Copy, scale=-SIXTEENTH)
+        nc.scalar.activation(wide[0][:, :last], banks[0][:, :last], ACT.Copy, scale=SIXTEENTH)
         far_c = [sig[t][:, 0:256] for t in range(PACK)]
         diff_c = [sig[t][:, 256:512] for t in range(PACK - 1)] + [z_woven[0][:].bitcast(F32)]
         woven1 = tile("z2_woven1", [P, 256 * PACK], BF16)[:]
         z2_piece(1, far_c, diff_c, woven1)
         z2_quantise(1, woven1)
         mx(banks[0][:, last:], z_q[0][:], z_s[0][:], z2_q[1][:], z2_s[1][:])
-        nc.scalar.activation(wide[0][:, last:S], banks[0][:, last:], ACT.Copy, scale=-SIXTEENTH)
+        nc.scalar.activation(wide[0][:, last:S], banks[0][:, last:], ACT.Copy, scale=SIXTEENTH)
         for u in range(1, PACK):
             nc.vector.quantize_mx(z_q[u][:].bitcast(FP8X4), z_s[u][:], z_woven[u][:])
             for n in range(len(PIECES)):
                 lo, hi = PIECES[n]
                 mx(banks[u][:, lo:hi], z_q[u][:], z_s[u][:], z2_q[n][:], z2_s[n][:])
-            nc.scalar.activation(wide[u][:, :S], banks[u][:], ACT.Copy, scale=-SIXTEENTH)
+            nc.scalar.activation(wide[u][:, :S], banks[u][:], ACT.Copy, scale=SIXTEENTH)
 
         out_rows = out.rearrange("(p u) v -> p u v", u=PACK)
-        g4 = [tile("g4_%d" % u, [P, S], F32) for u in range(PACK)]
-        low = [tile("low%d" % u, [P, S], F32) for u in range(PACK)]
-        v5 = [tile("v5_%d" % u, [P, S], F32) for u in range(PACK)]
-        v6 = [tile("v6_%d" % u, [P, S], F32) for u in range(PACK)]
-        res = [tile("res%d" % u, [P, S], F32) for u in range(PACK)]
+        g4, g5, g6, top, rise, lift, part, res = [
+            [tile("%s%d" % (name, u), [P, S], F32) for u in range(PACK)]
+            for name in ("g4_", "g5_", "g6_", "top", "rise", "lift", "part", "res")
+        ]
 
-        def first_pair_gather(u):
-            nc.vector.tensor_copy(g4[u][:], wide[u][:].indirect(n4_l[:]))
+        def fetch(dst, list_tile, u, lo, hi):
+            nc.vector.tensor_copy(dst[u][:, lo:hi], wide[u][:].indirect(list_tile[:, lo // 16 : hi // 16]))
 
-        def first_pair_min(u):
-            nc.vector.tensor_tensor(low[u][:], wide[u][:, :S], g4[u][:], ALU.min)
+        def first_max(u):
+            nc.vector.scalar_tensor_tensor(top[u][:], banks[u][:], SIXTEENTH, g4[u][:], ALU.mult, ALU.max)
 
-        def against(dst, list_tile, u, lo, hi):
-            nc.vector.tensor_tensor(dst[u][:, lo:hi], wide[u][:].indirect(list_tile[:, lo // 16 : hi // 16]), low[u][:, lo:hi], ALU.subtract)
-
-        def finish(u, lo, hi):
-            nc.vector.tensor_tensor(res[u][:, lo:hi], v5[u][:, lo:hi], v6[u][:, lo:hi], ALU.min)
-            nc.sync.dma_start(out_rows[:, u, lo:hi], res[u][:, lo:hi])
-
-        first_pair_gather(0)
-        first_pair_min(0)
         for u in range(PACK - 1):
-            against(v5, n5_l, u, 0, S)
-            first_pair_gather(u + 1)
-            against(v6, n6_l, u, 0, S)
-            first_pair_min(u + 1)
-            finish(u, 0, S)
+            fetch(g4, n4_l, u, 0, S)
+            fetch(g5, n5_l, u, 0, S)
+            first_max(u)
+            fetch(g6, n6_l, u, 0, S)
+            nc.gpsimd.tensor_tensor(part[u][:], top[u][:], g5[u][:], ALU.subtract)
+            nc.gpsimd.tensor_tensor(rise[u][:], g6[u][:], g5[u][:], ALU.subtract)
+            nc.scalar.activation(lift[u][:], rise[u][:], ACT.Relu)
+            nc.gpsimd.tensor_tensor(res[u][:], part[u][:], lift[u][:], ALU.subtract)
+            nc.sync.dma_start(out_rows[:, u, :], res[u][:])
         u, half = PACK - 1, S // 2
-        against(v5, n5_l, u, 0, half)
-        against(v6, n6_l, u, 0, half)
-        against(v5, n5_l, u, half, S)
-        finish(u, 0, half)
-        against(v6, n6_l, u, half, S)
-        finish(u, half, S)
+        fetch(g4, n4_l, u, 0, S)
+        fetch(g5, n5_l, u, 0, S)
+        first_max(u)
+        fetch(g6, n6_l, u, 0, half)
+        fetch(g6, n6_l, u, half, S)
+        for lo in (0, half):
+            nc.vector.tensor_tensor(rise[u][:, lo : lo + half], g5[u][:, lo : lo + half], g6[u][:, lo : lo + half], ALU.max)
+        for lo in (0, half):
+            nc.vector.tensor_tensor(res[u][:, lo : lo + half], top[u][:, lo : lo + half], rise[u][:, lo : lo + half], ALU.subtract)
+            nc.sync.dma_start(out_rows[:, u, lo : lo + half], res[u][:, lo : lo + half])

@@ -48,15 +48,15 @@ def tile_picked_ckqgatewindmix_none_p_kernel(
         ds_win = tile("ds_win", [P, G], U8)
         nc.gpsimd.memset(ds_win[:].bitcast(I32), 0)
         nc.gpsimd.memset(xs_win[:].bitcast(I32), 0)
+        k1_l = load_list("k1_l", k1)
         two_l = load_list("two_l", two)
+        nc.sync.dma_start(ds_win[0:P:8, :].bitcast(I32), d_scales[0].bitcast(I32))
         xw_win = tile("xw_win", [P, T], U32)
         nc.sync.dma_start(xw_win[:].bitcast(I32), x_words[0].rearrange("p n t -> p (n t)").bitcast(I32))
-        nc.sync.dma_start(ds_win[0:P:8, :].bitcast(I32), d_scales[0].bitcast(I32))
-        k1_l = load_list("k1_l", k1)
-        for q in range(4):
-            nc.sync.dma_start(xs_win[32 * q : 32 * q + 4, :].bitcast(I32), x_scales[0, 4 * q : 4 * q + 4, :].bitcast(I32))
         w_raw = tile("w_raw", [P, PACK, K], F32)
         nc.sync.dma_start(w_raw[:], w1.rearrange("(p j) c -> p j c", j=PACK))
+        for q in range(4):
+            nc.sync.dma_start(xs_win[32 * q : 32 * q + 4, :].bitcast(I32), x_scales[0, 4 * q : 4 * q + 4, :].bitcast(I32))
         offs_l = load_list("offs_l", offs)
         dw_win = tile("dw_win", [P, G], U32)
         nc.sync.dma_start(dw_win[:].bitcast(I32), d_words[0].rearrange("p n t -> p (n t)").bitcast(I32))
@@ -89,9 +89,8 @@ def tile_picked_ckqgatewindmix_none_p_kernel(
         x2_s = tile("x2_s", [P, S], U8)
         x1_w = tile("x1_w", [P, S], U32)
         x1_s = tile("x1_s", [P, S], U8)
-        nc.vector.tensor_copy(x2_w[:], xw_win[:].indirect(two_l[:]))
         nc.vector.tensor_copy(dk_s[:], ds_win[:].indirect(k1_l[:]))
-        nc.vector.tensor_copy(x2_s[:], xs_win[:].indirect(two_l[:]))
+        nc.vector.tensor_copy(x2_w[:], xw_win[:].indirect(two_l[:]))
         nc.vector.tensor_copy(
             dk_s_dealt[:].bitcast(I32).rearrange("p (t b r) -> p t b r", t=PACK, r=RUN // 4),
             dk_s[:].bitcast(I32).rearrange("p (b t r) -> p t b r", t=PACK, r=RUN // 4),
@@ -99,6 +98,7 @@ def tile_picked_ckqgatewindmix_none_p_kernel(
         for q in range(4):
             nc.sync.dma_start(ds_plane[32 * q : 32 * q + 4, :].bitcast(I32), dk_s_dealt[32 * q : 32 * q + 32 : 8, :].bitcast(I32))
         nc.vector.tensor_copy(x1_w[:], xw_win[:].indirect(offs_l[:]))
+        nc.vector.tensor_copy(x2_s[:], xs_win[:].indirect(two_l[:]))
         nc.vector.tensor_copy(x1_s[:], xs_win[:].indirect(offs_l[:]))
 
         w_cols = w_raw[:].rearrange("p j (b t r) -> p t b r j", t=PACK, r=RUN)
@@ -204,23 +204,30 @@ def tile_picked_ckqgatewindmix_none_p_kernel(
             nc.vector.scalar_tensor_tensor(top[u][:], banks[u][:], SIXTEENTH, g4[u][:], ALU.mult, ALU.max)
 
         for u in range(PACK - 1):
-            fetch(g4, n4_l, u, 0, S)
             fetch(g5, n5_l, u, 0, S)
-            first_max(u)
             fetch(g6, n6_l, u, 0, S)
-            nc.gpsimd.tensor_tensor(part[u][:], top[u][:], g5[u][:], ALU.subtract)
+            fetch(g4, n4_l, u, 0, S)
+            first_max(u)
             nc.gpsimd.tensor_tensor(rise[u][:], g6[u][:], g5[u][:], ALU.subtract)
             nc.scalar.activation(lift[u][:], rise[u][:], ACT.Relu)
+            nc.gpsimd.tensor_tensor(part[u][:], top[u][:], g5[u][:], ALU.subtract)
             nc.gpsimd.tensor_tensor(res[u][:], part[u][:], lift[u][:], ALU.subtract)
             nc.sync.dma_start(out_rows[:, u, :], res[u][:])
         u, half = PACK - 1, S // 2
+
+        def second_max(lo):
+            nc.vector.tensor_tensor(rise[u][:, lo : lo + half], g5[u][:, lo : lo + half], g6[u][:, lo : lo + half], ALU.max)
+
+        def finish(lo):
+            nc.vector.tensor_tensor(res[u][:, lo : lo + half], top[u][:, lo : lo + half], rise[u][:, lo : lo + half], ALU.subtract)
+            nc.sync.dma_start(out_rows[:, u, lo : lo + half], res[u][:, lo : lo + half])
+
         fetch(g4, n4_l, u, 0, S)
         fetch(g5, n5_l, u, 0, S)
         first_max(u)
         fetch(g6, n6_l, u, 0, half)
         fetch(g6, n6_l, u, half, S)
-        for lo in (0, half):
-            nc.vector.tensor_tensor(rise[u][:, lo : lo + half], g5[u][:, lo : lo + half], g6[u][:, lo : lo + half], ALU.max)
-        for lo in (0, half):
-            nc.vector.tensor_tensor(res[u][:, lo : lo + half], top[u][:, lo : lo + half], rise[u][:, lo : lo + half], ALU.subtract)
-            nc.sync.dma_start(out_rows[:, u, lo : lo + half], res[u][:, lo : lo + half])
+        second_max(0)
+        second_max(half)
+        finish(0)
+        finish(half)

@@ -50,6 +50,7 @@ def tile_picked_ckqgatewindmix_none_p_kernel(
         nc.gpsimd.memset(xs_win[:].bitcast(I32), 0)
         k1_l = load_list("k1_l", k1)
         two_l = load_list("two_l", two)
+        offs_l = load_list("offs_l", offs)
         nc.sync.dma_start(ds_win[0:P:8, :].bitcast(I32), d_scales[0].bitcast(I32))
         xw_win = tile("xw_win", [P, T], U32)
         nc.sync.dma_start(xw_win[:].bitcast(I32), x_words[0].rearrange("p n t -> p (n t)").bitcast(I32))
@@ -57,7 +58,6 @@ def tile_picked_ckqgatewindmix_none_p_kernel(
         nc.sync.dma_start(w_raw[:], w1.rearrange("(p j) c -> p j c", j=PACK))
         for q in range(4):
             nc.sync.dma_start(xs_win[32 * q : 32 * q + 4, :].bitcast(I32), x_scales[0, 4 * q : 4 * q + 4, :].bitcast(I32))
-        offs_l = load_list("offs_l", offs)
         dw_win = tile("dw_win", [P, G], U32)
         nc.sync.dma_start(dw_win[:].bitcast(I32), d_words[0].rearrange("p n t -> p (n t)").bitcast(I32))
         n3_l = load_list("n3_l", n3)

from contextlib import ExitStack

import concourse.mybir as mybir
from concourse.masks import make_identity

F32 = mybir.dt.float32
BF16 = mybir.dt.bfloat16
I32 = mybir.dt.int32
U32 = mybir.dt.uint32
U16 = mybir.dt.uint16
U8 = mybir.dt.uint8
FP8X4 = mybir.dt.float8_e4m3fn_x4
ALU = mybir.AluOpType
ACT = mybir.ActivationFunctionType

P = 128
PACK = 4
K, T, S, G = 512, 1024, 512, 2048
SIXTEENTH = 0.0625
PIECES = [(0, 256), (256, 512)]
RUN = 8
FLOPS = 3 * 2 * 512 * 512 * 512


def tile_picked_ckqgatewindmix_none_p_kernel(
    tc, x_words, x_scales, d_words, d_scales, w1, ga, gb, offs, k1, two, n1, n2, n3, n4, n5, n6, out
):
    nc = tc.nc
    with ExitStack() as ctx:
        lists = ctx.enter_context(tc.tile_pool(name="lists", bufs=1))
        keep = ctx.enter_context(tc.tile_pool(name="keep", bufs=1))
        psum = ctx.enter_context(tc.psum_pool(name="psum", bufs=1))

        def tile(name, shape, dtype):
            return keep.tile(shape, dtype, name=name, align_bytes=64)

        def load_list(name, src):
            held = lists.tile([P, S // 16], U16, name=name)
            nc.sync.dma_start(held[:], src)
            return held

        def mx(acc, lhs, lhs_scale, rhs, rhs_scale):
            nc.tensor.matmul_mx(acc, lhsT=lhs.bitcast(FP8X4), lhsT_scale=lhs_scale, rhs=rhs.bitcast(FP8X4), rhs_scale=rhs_scale, start=True, stop=True)

        banks = [psum.tile([P, S], F32, name="bank%d" % i) for i in range(8)]

        xs_win = tile("xs_win", [P, T], U8)
        ds_win = tile("ds_win", [P, G], U8)
        nc.gpsimd.memset(ds_win[:].bitcast(I32), 0)
        nc.gpsimd.memset(xs_win[:].bitcast(I32), 0)
        k1_l = load_list("k1_l", k1)
        two_l = load_list("two_l", two)
        offs_l = load_list("offs_l", offs)
        nc.sync.dma_start(ds_win[0:P:8, :].bitcast(I32), d_scales[0].bitcast(I32))
        xw_win = tile("xw_win", [P, T], U32)
        nc.sync.dma_start(xw_win[:].bitcast(I32), x_words[0].rearrange("p n t -> p (n t)").bitcast(I32))
        w_raw = tile("w_raw", [P, PACK, K], F32)
        nc.sync.dma_start(w_raw[:], w1.rearrange("(p j) c -> p j c", j=PACK))
        for q in range(4):
            nc.sync.dma_start(xs_win[32 * q : 32 * q + 4, :].bitcast(I32), x_scales[0, 4 * q : 4 * q + 4, :].bitcast(I32))
        dw_win = tile("dw_win", [P, G], U32)
        nc.sync.dma_start(dw_win[:].bitcast(I32), d_words[0].rearrange("p n t -> p (n t)").bitcast(I32))
        n3_l = load_list("n3_l", n3)
        n2_l = load_list("n2_l", n2)
        gain_rows = tile("gain_rows", [P, P], F32)
        nc.gpsimd.memset(gain_rows[:], 0.0)
        for i, gain in enumerate((ga, gb)):
            nc.sync.dma_start(
                gain_rows[PACK * i : PACK * (i + 1), :].rearrange("t (b r) -> t b r", r=RUN),
                gain.rearrange("(b t r) o -> t b (r o)", t=PACK, r=RUN),
            )
        n1_l = load_list("n1_l", n1)
        n4_l = load_list("n4_l", n4)
        n5_l = load_list("n5_l", n5)
        n6_l = load_list("n6_l", n6)

        ds_plane = tile("ds_plane", [P, S], U8)
        nc.gpsimd.memset(ds_plane[:].bitcast(I32), 0)
        identity = tile("identity", [P, P], F32)
        make_identity(nc, identity[:])
        wide = [tile("wide%d" % t, [P, 2 * S], F32) for t in range(PACK)]
        a_win = wide[: PACK - 1] + [tile("a_last", [P, 2 * S], F32)]
        for window in a_win + wide[PACK - 1 :]:
            nc.gpsimd.memset(window[:, S:], 0.0)

        dk_s = tile("dk_s", [P, S], U8)
        dk_s_dealt = tile("dk_s_dealt", [P, S], U8)
        x2_w = tile("x2_w", [P, S], U32)
        x2_s = tile("x2_s", [P, S], U8)
        x1_w = tile("x1_w", [P, S], U32)
        x1_s = tile("x1_s", [P, S], U8)
        nc.vector.tensor_copy(dk_s[:], ds_win[:].indirect(k1_l[:]))
        nc.vector.tensor_copy(x2_w[:], xw_win[:].indirect(two_l[:]))
        nc.vector.tensor_copy(
            dk_s_dealt[:].bitcast(I32).rearrange("p (t b r) -> p t b r", t=PACK, r=RUN // 4),
            dk_s[:].bitcast(I32).rearrange("p (b t r) -> p t b r", t=PACK, r=RUN // 4),
        )
        for q in range(4):
            nc.sync.dma_start(ds_plane[32 * q : 32 * q + 4, :].bitcast(I32), dk_s_dealt[32 * q : 32 * q + 32 : 8, :].bitcast(I32))
        nc.vector.tensor_copy(x1_w[:], xw_win[:].indirect(offs_l[:]))
        nc.vector.tensor_copy(x2_s[:], xs_win[:].indirect(two_l[:]))
        nc.vector.tensor_copy(x1_s[:], xs_win[:].indirect(offs_l[:]))

        w_cols = w_raw[:].rearrange("p j (b t r) -> p t b r j", t=PACK, r=RUN)
        b_win = [tile("b_win%d" % t, [P, S], F32) for t in range(PACK)]
        w_bf = [tile("w_bf%d" % t, [P, PACK * P], BF16) for t in range(PACK)]
        for t in range(PACK):
            nc.scalar.copy(w_bf[t][:].rearrange("p (b r j) -> p b r j", r=RUN, j=PACK), w_cols[:, t, :, :, :])
        for t in range(PACK):
            w_q = tile("w_q%d" % t, [P, P], U32)
            w_s = tile("w_s%d" % t, [P, P], U8)
            nc.vector.quantize_mx(w_q[:].bitcast(FP8X4), w_s[:], w_bf[t][:])
            mx(banks[t][:], w_q[:], w_s[:], x2_w[:], x2_s[:])
            nc.scalar.copy(b_win[t][:], banks[t][:])

        gains = tile("gains", [P, 2 * PACK], F32)
        nc.tensor.transpose(banks[7][:, :P], gain_rows[:], identity[:])
        nc.scalar.copy(gains[:], banks[7][:, : 2 * PACK])

        dk_w = tile("dk_w", [P, S], U32)
        dk_w_dealt = tile("dk_w_dealt", [P, S], U32)
        nc.vector.tensor_copy(dk_w[:], dw_win[:].indirect(k1_l[:]))
        nc.vector.tensor_copy(
            dk_w_dealt[:].rearrange("p (t b r) -> p t b r", t=PACK, r=RUN),
            dk_w[:].rearrange("p (b t r) -> p t b r", t=PACK, r=RUN),
        )
        sig = [tile("sig%d" % t, [P, S], F32) for t in range(PACK)]
        for t in range(PACK):
            cols = slice(P * t, P * (t + 1))
            mx(banks[4 + t][:], dk_w_dealt[:, cols], ds_plane[:, cols], x1_w[:], x1_s[:])
            nc.scalar.activation(a_win[t][:, :S], banks[4 + t][:], ACT.Copy, scale=SIXTEENTH)
            nc.scalar.activation(sig[t][:], a_win[t][:].indirect(n1_l[:]), ACT.Sigmoid)

        z2_q, z2_s = [], []

        def z2_piece(n, far, diff, woven):
            lo, hi = PIECES[n]
            width = hi - lo
            entries = slice(lo // 16, hi // 16)
            planes = tile("z2_planes%d" % n, [P, PACK, width], BF16)
            for step in range(PACK + 2):
                if step < PACK:
                    nc.vector.tensor_copy(far[step], b_win[step][:].indirect(n3_l[:, entries]))
                if 1 <= step < PACK + 1:
                    t = step - 1
                    nc.vector.tensor_tensor(diff[t], b_win[t][:].indirect(n2_l[:, entries]), far[t], ALU.subtract)
                if step >= 2:
                    t = step - 2
                    nc.vector.scalar_tensor_tensor(planes[:, t, :], b_win[t][:, lo:hi], gains[:, PACK + t : PACK + t + 1], diff[t], ALU.mult, ALU.mult)
            woven_view = woven.rearrange("p (c t) -> p c t", t=PACK)
            if n == len(PIECES) - 1:
                nc.vector.tensor_copy(woven_view, planes[:].rearrange("p t c -> p c t"))
            else:
                nc.scalar.copy(woven_view, planes[:].rearrange("p t c -> p c t"))
            z2_q.append(tile("z2_q%d" % n, [P, width], U32))
            z2_s.append(tile("z2_s%d" % n, [P, width], U8))

        def z2_quantise(n, woven):
            nc.vector.quantize_mx(z2_q[n][:].bitcast(FP8X4), z2_s[n][:], woven)

        def scratch(name, width):
            return [tile("%s%d" % (name, t), [P, width], F32)[:] for t in range(PACK)]

        woven0 = a_win[PACK - 1][:, S:].bitcast(BF16)
        z2_piece(0, scratch("far_a", 256), scratch("diff_a", 256), woven0)
        z_planes = tile("z_planes", [P, PACK, S], BF16)
        for t in range(PACK):
            nc.vector.scalar_tensor_tensor(z_planes[:, t, :], a_win[t][:, :S], gains[:, t : t + 1], sig[t][:], ALU.mult, ALU.mult)
        z_woven = [tile("z_woven%d" % u, [P, P * PACK], BF16) for u in range(PACK)]
        z_cols = z_planes[:].rearrange("p t (m u) -> p u m t", u=PACK)
        for u in range(PACK):
            nc.scalar.copy(z_woven[u][:].rearrange("p (m t) -> p m t", t=PACK), z_cols[:, u, :, :])
        z2_quantise(0, woven0)
        z_q = [tile("z_q%d" % u, [P, P], U32) for u in range(PACK)]
        z_s = [tile("z_s%d" % u, [P, P], U8) for u in range(PACK)]
        nc.vector.quantize_mx(z_q[0][:].bitcast(FP8X4), z_s[0][:], z_woven[0][:])
        last = PIECES[-1][0]
        mx(banks[0][:, :last], z_q[0][:], z_s[0][:], z2_q[0][:], z2_s[0][:])
        nc.scalar.activation(wide[0][:, :last], banks[0][:, :last], ACT.Copy, scale=SIXTEENTH)
        far_c = [sig[t][:, 0:256] for t in range(PACK)]
        diff_c = [sig[t][:, 256:512] for t in range(PACK - 1)] + [z_woven[0][:].bitcast(F32)]
        woven1 = tile("z2_woven1", [P, 256 * PACK], BF16)[:]
        z2_piece(1, far_c, diff_c, woven1)
        z2_quantise(1, woven1)
        mx(banks[0][:, last:], z_q[0][:], z_s[0][:], z2_q[1][:], z2_s[1][:])
        nc.scalar.activation(wide[0][:, last:S], banks[0][:, last:], ACT.Copy, scale=SIXTEENTH)
        for u in range(1, PACK):
            nc.vector.quantize_mx(z_q[u][:].bitcast(FP8X4), z_s[u][:], z_woven[u][:])
            for n in range(len(PIECES)):
                lo, hi = PIECES[n]
                mx(banks[u][:, lo:hi], z_q[u][:], z_s[u][:], z2_q[n][:], z2_s[n][:])
            nc.scalar.activation(wide[u][:, :S], banks[u][:], ACT.Copy, scale=SIXTEENTH)

        out_rows = out.rearrange("(p u) v -> p u v", u=PACK)
        g4, g5, g6, top, rise, lift, part, res = [
            [tile("%s%d" % (name, u), [P, S], F32) for u in range(PACK)]
            for name in ("g4_", "g5_", "g6_", "top", "rise", "lift", "part", "res")
        ]

        def fetch(dst, list_tile, u, lo, hi):
            nc.vector.tensor_copy(dst[u][:, lo:hi], wide[u][:].indirect(list_tile[:, lo // 16 : hi // 16]))

        def first_max(u):
            nc.vector.scalar_tensor_tensor(top[u][:], banks[u][:], SIXTEENTH, g4[u][:], ALU.mult, ALU.max)

        for u in range(PACK - 1):
            fetch(g5, n5_l, u, 0, S)
            fetch(g6, n6_l, u, 0, S)
            fetch(g4, n4_l, u, 0, S)
            first_max(u)
            nc.gpsimd.tensor_tensor(rise[u][:], g6[u][:], g5[u][:], ALU.subtract)
            nc.scalar.activation(lift[u][:], rise[u][:], ACT.Relu)
            nc.gpsimd.tensor_tensor(part[u][:], top[u][:], g5[u][:], ALU.subtract)
            nc.gpsimd.tensor_tensor(res[u][:], part[u][:], lift[u][:], ALU.subtract)
            nc.sync.dma_start(out_rows[:, u, :], res[u][:])
        u, half = PACK - 1, S // 2

        def second_max(lo):
            nc.vector.tensor_tensor(rise[u][:, lo : lo + half], g5[u][:, lo : lo + half], g6[u][:, lo : lo + half], ALU.max)

        def finish(lo):
            nc.vector.tensor_tensor(res[u][:, lo : lo + half], top[u][:, lo : lo + half], rise[u][:, lo : lo + half], ALU.subtract)
            nc.sync.dma_start(out_rows[:, u, lo : lo + half], res[u][:, lo : lo + half])

        fetch(g4, n4_l, u, 0, S)
        fetch(g5, n5_l, u, 0, S)
        first_max(u)
        fetch(g6, n6_l, u, 0, half)
        fetch(g6, n6_l, u, half, S)
        second_max(0)
        second_max(half)
        finish(0)
        finish(half)
